import numpy as np
import ml_dtypes


def mxq(x, axis, fmt="e4m3"):
    dtype, down = {"e4m3": (ml_dtypes.float8_e4m3fn, 7), "e5m2": (ml_dtypes.float8_e5m2, 14)}[fmt]
    v = np.moveaxis(np.asarray(x, np.float32).astype(ml_dtypes.bfloat16).astype(np.float64), axis, -1)
    blocks = v.reshape(v.shape[:-1] + (-1, 32))
    amax = np.abs(blocks).max(-1, keepdims=True)
    byte = np.maximum(np.where(amax > 0, np.frexp(amax)[1] - 1 + 127, 0) - down, 1)
    scale = np.exp2(byte - 127.0)
    codes = (blocks / scale).astype(np.float32).astype(dtype).astype(np.float64)
    return np.moveaxis((codes * scale).reshape(v.shape), -1, axis)


WIDE = False


def mx_kscale(k):
    if not WIDE:
        return np.ones(k)
    levels = np.array([10, -10, 5, -5, 0])
    if k % 512:
        return np.exp2(np.random.permutation(np.resize(levels, k // 32))).repeat(32)
    a = np.empty((k // 512, 16))
    for p in range(k // 512):
        a[p, :8] = np.random.permutation(np.resize(levels, 8))
        for g in range(8):
            far = levels[np.abs(levels - a[p, g]) >= 10]
            a[p, g + 8] = far[np.random.randint(len(far))]
    return np.exp2(a.ravel()).repeat(32)


def f64(x):
    return np.asarray(x).astype(np.float64)


def striped(idx):
    return np.tile(np.asarray(idx).reshape(-1, 16).T, (8, 1)).astype(np.uint16)


def unstriped(offs):
    return offs[:16].T.reshape(-1).astype(np.int64)


E2M1 = np.array([0.0, 0.5, 1.0, 1.5, 2.0, 3.0, 4.0, 6.0, -0.0, -0.5, -1.0, -1.5, -2.0, -3.0, -4.0, -6.0])


def pack_weight(w, fmt):
    k, n = w.shape
    w = f64(np.asarray(w, np.float32).astype(ml_dtypes.bfloat16)).reshape(k // 32, 32, n)
    amax = np.abs(w).max(1)
    if fmt == "e4m3":
        byte = np.frexp(amax)[1] - 1 + 127 - 7
    else:
        mant, ex = np.frexp(amax / 6.0)
        byte = np.where(mant > 0.5, ex, ex - 1) + 127
    byte = np.clip(np.where(amax > 0, byte, 1), 1, 254)
    scaled = (w * np.exp2(127.0 - byte)[:, None, :]).reshape(k, n).astype(np.float32)
    by_word = np.ascontiguousarray(scaled.reshape(k // 512, 128, 4, n).transpose(0, 1, 3, 2))
    if fmt == "e4m3":
        words = by_word.astype(ml_dtypes.float8_e4m3fn).view(np.uint8)
    else:
        c = by_word.astype(ml_dtypes.float4_e2m1fn).view(np.uint8) & 0xF
        words = (c[..., 0::2] | (c[..., 1::2] << 4)).reshape(k // 512, 128, 2 * n)
    return np.ascontiguousarray(words), np.ascontiguousarray(byte.astype(np.uint8).reshape(k // 512, 16, n))


def unpack_weight(words, scales, fmt):
    g, _, n = scales.shape
    words = np.ascontiguousarray(words).reshape(g, 128, n, -1)
    if fmt == "e4m3":
        vals = words.view(ml_dtypes.float8_e4m3fn).astype(np.float64)
    else:
        nib = np.empty((g, 128, n, 4), np.uint8)
        nib[..., 0::2] = words & 0xF
        nib[..., 1::2] = words >> 4
        vals = E2M1[nib]
    vals = vals * np.repeat(np.exp2(scales.astype(np.float64) - 127.0), 8, axis=1)[..., None]
    return vals.transpose(0, 1, 3, 2).reshape(g * 512, n)


def bf(x):
    return np.asarray(x, np.float32).astype(ml_dtypes.bfloat16)


def planes(Y):
    r, m = Y.shape
    b = f64(bf(Y)).reshape(r // 32, 32, m)
    amax = np.abs(b).max(1)
    byte = np.clip(np.where(amax > 0, np.frexp(amax)[1] - 1 + 127 - 7, 1), 1, 254)
    codes = (b * np.exp2(127.0 - byte)[:, None, :]).reshape(r, m).astype(np.float32).astype(ml_dtypes.float8_e4m3fn).view(np.uint8)
    words = codes.reshape(r // 512, 128, 4, m).transpose(0, 1, 3, 2)
    return np.ascontiguousarray(words), np.ascontiguousarray(byte.astype(np.uint8).reshape(r // 512, 16, m))


D, T, I, Q, E, Z, C = 512, 2048, 512, 512, 512, 1024, 256


def setup_inputs():
    n = np.random.standard_normal
    idx = np.random.permutation(T)[:I]
    idx2 = np.random.permutation(Z)[:I]
    idx3 = np.random.permutation(Z)[:I]
    idx4 = np.random.permutation(Q)[:C]
    fd = mx_kscale(D)
    fi = mx_kscale(I)
    ti = np.ones(T)
    ti[idx] = fi
    keysp = pack_weight(n((D, T)) / fd[:, None], "e2m1")
    return {
        "query": (n((D, Q)) * 1.0 / np.sqrt(D) * fd[:, None]).astype(np.float32),
        "keys_words": keysp[0],
        "keys_scales": keysp[1],
        "os": (np.random.uniform(0.02, 0.08, (1, I)) * fi).astype(np.float32),
        "vals": (n((E, T)) / ti).astype(np.float32),
        "pgain": (np.random.uniform(0.5, 2.0, (1, C))).astype(np.float32),
        "offs": striped(idx),
        "offs2": striped(idx2),
        "offs3": striped(idx3),
        "offs4": striped(idx4),
    }


def reference(query, keys_words, keys_scales, os, vals, pgain, offs, offs2, offs3, offs4):
    idx = unstriped(offs)
    idx2 = unstriped(offs2)
    idx3 = unstriped(offs3)
    idx4 = unstriped(offs4)
    keysu = unpack_weight(keys_words, keys_scales, "e2m1")
    queryq = mxq(f64(query), 0, "e4m3")
    keysidxg = keysu[:, idx]
    a = queryq.T @ keysidxg
    f0 = np.zeros((Q, Z))
    f0[:, idx2] = a
    s = a + f0[:, idx3]
    w = np.maximum(s, 0.0)
    wo1 = w * f64(os)
    wt1 = wo1.T
    vt1 = f64(vals)[:, idx].T
    vt1q = mxq(vt1, 0, "e4m3")
    wt1q = mxq(wt1, 0, "e4m3")
    o = vt1q.T @ wt1q
    y = o[:, idx4] * f64(pgain)
    words, scales = planes(y)
    return y, words, scales

@@ -1,0 +1,249 @@
+from contextlib import ExitStack
+
+import concourse.mybir as mybir
+from concourse.masks import make_identity
+
+D, T, I, Q, E, Z, C = 512, 2048, 512, 512, 512, 1024, 256
+FLOPS = 2 * D * Q * I + 2 * I * E * Q
+
+F32 = mybir.dt.float32
+BF16 = mybir.dt.bfloat16
+I32 = mybir.dt.int32
+U32 = mybir.dt.uint32
+U16 = mybir.dt.uint16
+U8 = mybir.dt.uint8
+FP8X4 = mybir.dt.float8_e4m3fn_x4
+FP4X4 = mybir.dt.float4_e2m1fn_x4
+ALU = mybir.AluOpType
+COPY = mybir.ActivationFunctionType.Copy
+
+P = 128
+PACK = 4
+STRIPE = 16
+TILES = Q // P
+HALF = I // 2
+SPLIT = 256
+WINDOWS = 3
+
+
+def tile_attend_passedthrough_pickedout_lean_pl_kernel(
+    tc, query, keys_words, keys_scales, slot_factor, vals, pgain, offs, offs2, offs3, offs4, out_0, out_1, out_2
+):
+    nc = tc.nc
+    with ExitStack() as ctx:
+        lists = ctx.enter_context(tc.tile_pool(name="lists", bufs=1))
+        sb = ctx.enter_context(tc.tile_pool(name="sb", bufs=1))
+        psum = ctx.enter_context(tc.psum_pool(name="psum", bufs=1))
+
+        def bank(b, shape):
+            return psum.tile([P] + shape, F32, name=f"bank{b}")
+
+        def entries(tile, a, b):
+            return tile[:, a // STRIPE : b // STRIPE]
+
+        def interleave(copy, dst, src):
+            copy(dst.rearrange("p (c i) t -> p c t i", i=4), src.rearrange("p t (c i) -> p c t i", i=4))
+
+        def quantize(codes, scales, grouped):
+            nc.vector.quantize_mx(out=codes.bitcast(FP8X4), scales=scales, in_=grouped.rearrange("p c t -> p (c t)"))
+
+        idx = lists.tile([P, I // STRIPE], U16, name="idx")
+        idx2 = lists.tile([P, I // STRIPE], U16, name="idx2")
+        idx3 = lists.tile([P, I // STRIPE], U16, name="idx3")
+        idx4 = lists.tile([P, C // STRIPE], U16, name="idx4")
+
+        key_words = sb.tile([P, T], U16, name="key_words")
+        key_scales = sb.tile([P, T], U8, name="key_scales")
+        q_first = sb.tile([P, PACK, P], F32, name="q_first")
+        q_rest = sb.tile([P, PACK, Q - P], F32, name="q_rest")
+        factor = sb.tile([P, PACK], F32, name="factor")
+        gain = sb.tile([P, C], F32, name="gain")
+        val_rows = [sb.tile([P, T], F32, name=f"val_rows{j}", align_bytes=64) for j in range(PACK)]
+        f0 = [sb.tile([P, Z], F32, name=f"f0_{k}") for k in range(WINDOWS)]
+        ident = sb.tile([P, P], F32, name="ident")
+
+        nc.gpsimd.memset(key_scales[:].bitcast(I32), 0)
+        for k in range(WINDOWS):
+            nc.vector.memset(f0[k][:], 0.0)
+        make_identity(nc, ident[:])
+
+        q_rows = query.rearrange("(p j) q -> p j q", j=PACK)
+        val_dealt = vals.rearrange("(p j) t -> p j t", j=PACK)
+        nc.sync.dma_start(idx[:], offs)
+        nc.sync.dma_start(idx2[:], offs2)
+        nc.scalar.dma_start(q_first[:], q_rows[:, :, 0:P])
+        for g in range(4):
+            queue = nc.sync if g % 2 == 0 else nc.scalar
+            queue.dma_start(
+                key_scales[32 * g : 32 * g + 4, :].bitcast(I32), keys_scales[0, 4 * g : 4 * g + 4, :].bitcast(I32)
+            )
+        nc.sync.dma_start(key_words[:].bitcast(I32), keys_words[0].bitcast(I32))
+        nc.sync.dma_start(q_rest[:], q_rows[:, :, P:Q])
+        nc.sync.dma_start(idx3[:], offs3)
+        nc.sync.dma_start(factor[:], slot_factor[0].rearrange("(p t) -> p t", t=PACK))
+        for j in range(PACK):
+            nc.sync.dma_start(val_rows[j][:], val_dealt[:, j, :])
+        nc.sync.dma_start(idx4[:], offs4)
+        nc.sync.dma_start(gain[:], pgain[0].partition_broadcast(P))
+
+        k_codes = sb.tile([P, I], U16, name="k_codes", align_bytes=64)
+        k_scales = sb.tile([P, I], U8, name="k_scales", align_bytes=64)
+        q_codes = sb.tile([P, Q], U32, name="q_codes", align_bytes=64)
+        q_scales = sb.tile([P, Q], U8, name="q_scales", align_bytes=64)
+        w_codes = sb.tile([P, Q], U32, name="w_codes", align_bytes=64)
+        w_scales = sb.tile([P, Q], U8, name="w_scales", align_bytes=64)
+        v_codes = sb.tile([P, E], U32, name="v_codes", align_bytes=64)
+        v_scales = sb.tile([P, E], U8, name="v_scales", align_bytes=64)
+        a = [sb.tile([P, (HALF, SPLIT, I, I)[n]], F32, name=f"a{n}", align_bytes=64) for n in range(TILES)]
+        a_bank = [bank(n, [I]) for n in range(TILES)]
+
+        def gather_key_words(lo, hi):
+            nc.vector.tensor_copy(k_codes[:, lo:hi], key_words[:].indirect(entries(idx, lo, hi)))
+
+        def quantize_queries(copy, src, lo, hi):
+            grouped = sb.tile([P, hi - lo, PACK], BF16, name="q_grouped", align_bytes=64)
+            interleave(copy, grouped[:], src)
+            quantize(q_codes[:, lo:hi], q_scales[:, lo:hi], grouped[:])
+
+        def score(n, lo, hi):
+            rows = slice(n * P, (n + 1) * P)
+            nc.tensor.matmul_mx(
+                out=a_bank[n][:, lo:hi],
+                lhsT=q_codes[:, rows].bitcast(FP8X4),
+                lhsT_scale=q_scales[:, rows],
+                rhs=k_codes[:, lo:hi].bitcast(FP4X4),
+                rhs_scale=k_scales[:, lo:hi],
+                start=True,
+                stop=True,
+            )
+
+        def scatter_scalar(n, lo, hi):
+            nc.scalar.activation(f0[n % WINDOWS][:].indirect(entries(idx2, lo, hi)), a[n][:, lo:hi], COPY)
+
+        def scatter_vector(n, lo, hi, source):
+            nc.vector.tensor_copy(f0[n % WINDOWS][:].indirect(entries(idx2, lo, hi)), source)
+
+        def look_up(n, name, parts):
+            s = sb.tile([P, I], F32, name=name, align_bytes=64)
+            for lo, hi, source in parts:
+                nc.vector.tensor_tensor(s[:, lo:hi], f0[n % WINDOWS][:].indirect(entries(idx3, lo, hi)), source, ALU.add)
+            turned = bank(4 + n % 2, [PACK, P])
+            for t in range(PACK):
+                nc.tensor.transpose(turned[:, t, :], s[:, t:I:PACK], ident[:])
+            return turned
+
+        def weigh(n, turned, name):
+            grouped = sb.tile([P, P, PACK], BF16, name=name, align_bytes=64)
+            nc.vector.scalar_tensor_tensor(
+                out=grouped[:],
+                in0=turned[:].rearrange("p t q -> p q t"),
+                scalar=0.0,
+                in1=factor[:].unsqueeze(1).to_broadcast([P, P, PACK]),
+                op0=ALU.max,
+                op1=ALU.mult,
+            )
+            cols = slice(n * P, (n + 1) * P)
+            quantize(w_codes[:, cols], w_scales[:, cols], grouped[:])
+
+        def pick_values(j, picked, turned):
+            if j == 0:
+                nc.vector.tensor_copy(picked, val_rows[j][:].indirect(idx[:]))
+            else:
+                nc.scalar.activation(picked, val_rows[j][:].indirect(idx[:]), COPY)
+            pairs = picked.bitcast(F32)
+            for u in range(2):
+                nc.tensor.transpose(turned[:, j % 2, u, :], pairs[:, u : I // 2 : 2], ident[:])
+
+        def quantize_values(j, turned, name):
+            grouped = sb.tile([P, 2 * P, PACK], BF16, name=name, align_bytes=64)
+            nc.scalar.copy(
+                grouped[:].bitcast(F32).rearrange("p (j m) u -> p j m u", j=2), turned[:].rearrange("p j u m -> p j m u")
+            )
+            cols = slice(j * P, (j + 2) * P)
+            quantize(v_codes[:, cols], v_scales[:, cols], grouped[:])
+
+        def weighted_sum(out, j, lo, hi):
+            cols = slice(j * P, (j + 1) * P)
+            nc.tensor.matmul_mx(
+                out=out,
+                lhsT=v_codes[:, cols].bitcast(FP8X4),
+                lhsT_scale=v_scales[:, cols],
+                rhs=w_codes[:, lo:hi].bitcast(FP8X4),
+                rhs_scale=w_scales[:, lo:hi],
+                start=True,
+                stop=True,
+            )
+
+        nc.vector.tensor_copy(k_scales[:], key_scales[:].indirect(idx[:]))
+        gather_key_words(0, HALF)
+        quantize_queries(nc.scalar.copy, q_first[:], 0, P)
+        score(0, 0, HALF)
+        nc.scalar.copy(a[0][:, 0:HALF], a_bank[0][:, 0:HALF])
+        scatter_scalar(0, 0, HALF)
+        gather_key_words(HALF, I)
+        score(0, HALF, I)
+        quantize_queries(nc.vector.tensor_copy, q_rest[:, :, 0:P], P, 2 * P)
+        score(1, 0, I)
+        quantize_queries(nc.vector.tensor_copy, q_rest[:, :, P : Q - P], 2 * P, Q)
+        score(2, 0, I)
+        score(3, 0, I)
+        a0_rest = sb.tile([P, HALF], F32, name="q_grouped", align_bytes=64)
+        nc.vector.tensor_copy(a0_rest[:], a_bank[0][:, HALF:I])
+        scatter_vector(0, HALF, I, a0_rest[:])
+        turned0 = look_up(0, "s0", [(0, HALF, a[0][:]), (HALF, I, a0_rest[:])])
+        nc.scalar.copy(a[1][:], a_bank[1][:, 0:SPLIT])
+        scatter_scalar(1, 0, SPLIT)
+        a1_rest = sb.tile([P, I - SPLIT], F32, name="q_grouped", align_bytes=64)
+        nc.vector.tensor_copy(a1_rest[:], a_bank[1][:, SPLIT:I])
+        scatter_vector(1, SPLIT, I, a1_rest[:])
+        turned1 = look_up(1, "s1", [(0, SPLIT, a[1][:]), (SPLIT, I, a1_rest[:])])
+        weigh(0, turned0, "w_grouped0")
+        nc.scalar.copy(a[2][:], a_bank[2][:])
+        scatter_scalar(2, 0, HALF)
+        scatter_scalar(2, HALF, I)
+        turned2 = look_up(2, "w_grouped0", [(0, I, a[2][:])])
+        v_turned = [bank(6, [2, 2, P]), bank(7, [2, 2, P])]
+        picked0 = sb.tile([P, I], BF16, name="picked0", align_bytes=64)
+        pick_values(0, picked0[:], v_turned[0])
+        weigh(1, turned1, "picked0")
+        nc.scalar.copy(a[3][:], a_bank[3][:])
+        scatter_scalar(3, 0, HALF)
+        scatter_scalar(3, HALF, I)
+        turned3 = look_up(3, "picked0", [(0, I, a[3][:])])
+        weigh(2, turned2, "w_grouped2")
+        picked = sb.tile([P, 3 * I], BF16, name="a2", align_bytes=64)
+        pick_values(1, picked[:, 0:I], v_turned[0])
+        pick_values(2, picked[:, I : 2 * I], v_turned[1])
+        pick_values(3, picked[:, 2 * I : 3 * I], v_turned[1])
+        weigh(3, turned3, "w_grouped3")
+        quantize_values(0, v_turned[0], "val_rows3")
+        quantize_values(2, v_turned[1], "v_grouped2")
+
+        o = [sb.tile([P, Q], F32, name=f"o{j}") for j in range(PACK)]
+        for j in range(PACK):
+            sums = bank(j, [Q])
+            weighted_sum(sums[:], j, 0, Q)
+            copy = nc.vector.tensor_copy if j == 1 else nc.scalar.copy
+            copy(o[j][:], sums[:])
+        y = sb.tile([P, PACK, C], F32, name="y")
+        looked_up = sb.tile([P, C], F32, name="looked_up")
+        out_rows = out_0.rearrange("(p j) c -> p j c", j=PACK)
+        for j in range(PACK - 1):
+            nc.vector.tensor_tensor(y[:, j, :], o[j][:].indirect(idx4[:]), gain[:], ALU.mult)
+            if j == 1:
+                nc.sync.dma_start(out_rows[:, 0:2, :], y[:, 0:2, :])
+        nc.scalar.activation(looked_up[:], o[3][:].indirect(idx4[:]), COPY)
+        nc.vector.tensor_tensor(y[:, 3, :], looked_up[:], gain[:], ALU.mult)
+        nc.sync.dma_start(out_rows[:, 2:4, :], y[:, 2:4, :])
+
+        y_grouped = sb.tile([P, C, PACK], BF16, name="y_grouped", align_bytes=64)
+        y_codes = sb.tile([P, C], U32, name="y_codes", align_bytes=64)
+        y_scales = sb.tile([P, C], U8, name="y_scales", align_bytes=64)
+        interleave(nc.vector.tensor_copy, y_grouped[:], y[:])
+        quantize(y_codes[:], y_scales[:], y_grouped[:])
+        nc.sync.dma_start(out_1[0].rearrange("p c t -> p (c t)").bitcast(I32), y_codes[:].bitcast(I32))
+        for g in range(4):
+            queue = nc.sync if g % 2 == 0 else nc.scalar
+            queue.dma_start(
+                out_2[0, 4 * g : 4 * g + 4, :].bitcast(I32), y_scales[32 * g : 32 * g + 4, :].bitcast(I32)
+            )

@@ -22,8 +22,7 @@ PACK = 4
 STRIPE = 16
 TILES = Q // P
 HALF = I // 2
-SPLIT = 256
-WINDOWS = 3
+SCALAR_COLUMNS = 96
 
 
 def tile_attend_passedthrough_pickedout_lean_pl_kernel(
@@ -54,18 +53,19 @@ def tile_attend_passedthrough_pickedout_lean_pl_kernel(
 
         key_words = sb.tile([P, T], U16, name="key_words")
         key_scales = sb.tile([P, T], U8, name="key_scales")
-        q_first = sb.tile([P, PACK, P], F32, name="q_first")
+        q_first = sb.tile([P, PACK, P], F32, name="q_first", align_bytes=64)
         q_rest = sb.tile([P, PACK, Q - P], F32, name="q_rest")
         factor = sb.tile([P, PACK], F32, name="factor")
         gain = sb.tile([P, C], F32, name="gain")
         val_rows = [sb.tile([P, T], F32, name=f"val_rows{j}", align_bytes=64) for j in range(PACK)]
-        f0 = [sb.tile([P, Z], F32, name=f"f0_{k}") for k in range(WINDOWS)]
+        f0 = [sb.tile([P, Z], F32, name=f"f0_{n}", align_bytes=64) for n in range(TILES)]
         ident = sb.tile([P, P], F32, name="ident")
 
         nc.gpsimd.memset(key_scales[:].bitcast(I32), 0)
-        for k in range(WINDOWS):
-            nc.vector.memset(f0[k][:], 0.0)
+        for n in range(TILES - 1):
+            nc.vector.memset(f0[n][:], 0.0)
         make_identity(nc, ident[:])
+        nc.gpsimd.memset(f0[TILES - 1][:], 0.0)
 
         q_rows = query.rearrange("(p j) q -> p j q", j=PACK)
         val_dealt = vals.rearrange("(p j) t -> p j t", j=PACK)
@@ -79,167 +79,148 @@ def tile_attend_passedthrough_pickedout_lean_pl_kernel(
             )
         nc.sync.dma_start(key_words[:].bitcast(I32), keys_words[0].bitcast(I32))
         nc.sync.dma_start(q_rest[:], q_rows[:, :, P:Q])
-        nc.sync.dma_start(idx3[:], offs3)
-        nc.sync.dma_start(factor[:], slot_factor[0].rearrange("(p t) -> p t", t=PACK))
         for j in range(PACK):
             nc.sync.dma_start(val_rows[j][:], val_dealt[:, j, :])
+            if j == 1:
+                nc.sync.dma_start(idx3[:], offs3)
+                nc.sync.dma_start(factor[:], slot_factor[0].rearrange("(p t) -> p t", t=PACK))
         nc.sync.dma_start(idx4[:], offs4)
         nc.sync.dma_start(gain[:], pgain[0].partition_broadcast(P))
 
-        k_codes = sb.tile([P, I], U16, name="k_codes", align_bytes=64)
-        k_scales = sb.tile([P, I], U8, name="k_scales", align_bytes=64)
         q_codes = sb.tile([P, Q], U32, name="q_codes", align_bytes=64)
         q_scales = sb.tile([P, Q], U8, name="q_scales", align_bytes=64)
         w_codes = sb.tile([P, Q], U32, name="w_codes", align_bytes=64)
         w_scales = sb.tile([P, Q], U8, name="w_scales", align_bytes=64)
+        w_grouped = sb.tile([P, Q, PACK], BF16, name="w_grouped", align_bytes=64)
         v_codes = sb.tile([P, E], U32, name="v_codes", align_bytes=64)
         v_scales = sb.tile([P, E], U8, name="v_scales", align_bytes=64)
-        a = [sb.tile([P, (HALF, SPLIT, I, I)[n]], F32, name=f"a{n}", align_bytes=64) for n in range(TILES)]
+        k_scales = sb.tile([P, I], U8, name="k_scales", align_bytes=64)
         a_bank = [bank(n, [I]) for n in range(TILES)]
+        a = {n: sb.tile([P, I], F32, name=f"a{n}") for n in (0, 1, 3)}
 
-        def gather_key_words(lo, hi):
-            nc.vector.tensor_copy(k_codes[:, lo:hi], key_words[:].indirect(entries(idx, lo, hi)))
+        def gather_key_words(h, name):
+            codes = sb.tile([P, HALF], U16, name=name, align_bytes=64)
+            nc.vector.tensor_copy(codes[:], key_words[:].indirect(entries(idx, h * HALF, (h + 1) * HALF)))
+            return codes
 
-        def quantize_queries(copy, src, lo, hi):
-            grouped = sb.tile([P, hi - lo, PACK], BF16, name="q_grouped", align_bytes=64)
+        def round_queries(copy, src, name):
+            grouped = sb.tile([P, src.shape[2], PACK], BF16, name=name, align_bytes=64)
             interleave(copy, grouped[:], src)
-            quantize(q_codes[:, lo:hi], q_scales[:, lo:hi], grouped[:])
+            return grouped
 
-        def score(n, lo, hi):
+        def score(n, h):
             rows = slice(n * P, (n + 1) * P)
             nc.tensor.matmul_mx(
-                out=a_bank[n][:, lo:hi],
+                out=a_bank[n][:, h * HALF : (h + 1) * HALF],
                 lhsT=q_codes[:, rows].bitcast(FP8X4),
                 lhsT_scale=q_scales[:, rows],
-                rhs=k_codes[:, lo:hi].bitcast(FP4X4),
-                rhs_scale=k_scales[:, lo:hi],
+                rhs=k_codes[h][:].bitcast(FP4X4),
+                rhs_scale=k_scales[:, h * HALF : (h + 1) * HALF],
                 start=True,
                 stop=True,
             )
 
         def scatter_scalar(n, lo, hi):
-            nc.scalar.activation(f0[n % WINDOWS][:].indirect(entries(idx2, lo, hi)), a[n][:, lo:hi], COPY)
+            nc.scalar.activation(f0[n][:].indirect(entries(idx2, lo, hi)), a[n][:, lo:hi], COPY)
 
-        def scatter_vector(n, lo, hi, source):
-            nc.vector.tensor_copy(f0[n % WINDOWS][:].indirect(entries(idx2, lo, hi)), source)
-
-        def look_up(n, name, parts):
-            s = sb.tile([P, I], F32, name=name, align_bytes=64)
-            for lo, hi, source in parts:
-                nc.vector.tensor_tensor(s[:, lo:hi], f0[n % WINDOWS][:].indirect(entries(idx3, lo, hi)), source, ALU.add)
-            turned = bank(4 + n % 2, [PACK, P])
+        def look_up(n):
+            s = sb.tile([P, I], F32, name=f"s{n}")
+            nc.vector.tensor_tensor(s[:], f0[n][:].indirect(idx3[:]), a[n][:], ALU.add)
+            turned = bank(n, [PACK, P])
             for t in range(PACK):
                 nc.tensor.transpose(turned[:, t, :], s[:, t:I:PACK], ident[:])
             return turned
 
-        def weigh(n, turned, name):
-            grouped = sb.tile([P, P, PACK], BF16, name=name, align_bytes=64)
+        def weigh(n, turned):
             nc.vector.scalar_tensor_tensor(
-                out=grouped[:],
+                out=w_grouped[:, n * P : (n + 1) * P, :],
                 in0=turned[:].rearrange("p t q -> p q t"),
                 scalar=0.0,
                 in1=factor[:].unsqueeze(1).to_broadcast([P, P, PACK]),
                 op0=ALU.max,
                 op1=ALU.mult,
             )
-            cols = slice(n * P, (n + 1) * P)
-            quantize(w_codes[:, cols], w_scales[:, cols], grouped[:])
 
-        def pick_values(j, picked, turned):
-            if j == 0:
-                nc.vector.tensor_copy(picked, val_rows[j][:].indirect(idx[:]))
+        def pick_values(j, name):
+            picked = sb.tile([P, I], BF16, name=name, align_bytes=64)
+            if j >= 1:
+                nc.scalar.activation(picked[:], val_rows[j][:].indirect(idx[:]), COPY)
             else:
-                nc.scalar.activation(picked, val_rows[j][:].indirect(idx[:]), COPY)
-            pairs = picked.bitcast(F32)
+                nc.vector.tensor_copy(picked[:], val_rows[j][:].indirect(idx[:]))
+            pairs = picked[:].bitcast(F32)
             for u in range(2):
-                nc.tensor.transpose(turned[:, j % 2, u, :], pairs[:, u : I // 2 : 2], ident[:])
+                nc.tensor.transpose(v_turned[j // 2][:, j % 2, u, :], pairs[:, u : I // 2 : 2], ident[:])
 
-        def quantize_values(j, turned, name):
+        def quantize_values(j, name):
             grouped = sb.tile([P, 2 * P, PACK], BF16, name=name, align_bytes=64)
             nc.scalar.copy(
-                grouped[:].bitcast(F32).rearrange("p (j m) u -> p j m u", j=2), turned[:].rearrange("p j u m -> p j m u")
+                grouped[:].bitcast(F32).rearrange("p (j m) u -> p j m u", j=2),
+                v_turned[j // 2][:].rearrange("p j u m -> p j m u"),
             )
             cols = slice(j * P, (j + 2) * P)
             quantize(v_codes[:, cols], v_scales[:, cols], grouped[:])
 
-        def weighted_sum(out, j, lo, hi):
+        nc.vector.tensor_copy(k_scales[:], key_scales[:].indirect(idx[:]))
+        k_codes = [gather_key_words(0, "k_codes")]
+        grouped = round_queries(nc.scalar.copy, q_first[:], "q_grouped0")
+        quantize(q_codes[:, 0:P], q_scales[:, 0:P], grouped[:])
+        score(0, 0)
+        nc.scalar.copy(a[0][:, 0:HALF], a_bank[0][:, 0:HALF])
+        scatter_scalar(0, 0, HALF)
+        k_codes.append(gather_key_words(1, "q_first"))
+        score(0, 1)
+        nc.scalar.copy(a[0][:, HALF:I], a_bank[0][:, HALF:I])
+        scatter_scalar(0, HALF, I)
+        grouped = round_queries(nc.vector.tensor_copy, q_rest[:], "q_grouped1")
+        quantize(q_codes[:, P:Q], q_scales[:, P:Q], grouped[:])
+        for n in (2, 1, 3):
+            score(n, 0)
+            score(n, 1)
+        v_turned = [bank(4, [2, 2, P]), bank(5, [2, 2, P])]
+        pick_values(0, "picked0")
+        a[2] = sb.tile([P, I], F32, name="val_rows0", align_bytes=64)
+        nc.vector.tensor_copy(a[2][:], a_bank[2][:])
+        nc.vector.tensor_copy(a[3][:], a_bank[3][:])
+        nc.vector.tensor_copy(f0[2][:].indirect(idx2[:]), a[2][:])
+        nc.scalar.copy(a[1][:], a_bank[1][:])
+        for n in (1, 3):
+            scatter_scalar(n, 0, HALF)
+            scatter_scalar(n, HALF, I)
+        turned = {n: look_up(n) for n in (0, 2, 1, 3)}
+        for n in turned:
+            weigh(n, turned[n])
+        quantize(w_codes[:], w_scales[:], w_grouped[:])
+        pick_values(1, "val_rows0")
+        pick_values(2, "picked2")
+        pick_values(3, "picked3")
+        quantize_values(0, "val_rows3")
+        quantize_values(2, "v_grouped")
+
+        y = sb.tile([P, PACK, C], F32, name="y")
+        out_rows = out_0.rearrange("(p j) c -> p j c", j=PACK)
+        for j in range(PACK):
+            sums = bank((6, 7, 0, 1)[j], [Q])
             cols = slice(j * P, (j + 1) * P)
             nc.tensor.matmul_mx(
-                out=out,
+                out=sums[:],
                 lhsT=v_codes[:, cols].bitcast(FP8X4),
                 lhsT_scale=v_scales[:, cols],
-                rhs=w_codes[:, lo:hi].bitcast(FP8X4),
-                rhs_scale=w_scales[:, lo:hi],
+                rhs=w_codes[:].bitcast(FP8X4),
+                rhs_scale=w_scales[:],
                 start=True,
                 stop=True,
             )
-
-        nc.vector.tensor_copy(k_scales[:], key_scales[:].indirect(idx[:]))
-        gather_key_words(0, HALF)
-        quantize_queries(nc.scalar.copy, q_first[:], 0, P)
-        score(0, 0, HALF)
-        nc.scalar.copy(a[0][:, 0:HALF], a_bank[0][:, 0:HALF])
-        scatter_scalar(0, 0, HALF)
-        gather_key_words(HALF, I)
-        score(0, HALF, I)
-        quantize_queries(nc.vector.tensor_copy, q_rest[:, :, 0:P], P, 2 * P)
-        score(1, 0, I)
-        quantize_queries(nc.vector.tensor_copy, q_rest[:, :, P : Q - P], 2 * P, Q)
-        score(2, 0, I)
-        score(3, 0, I)
-        a0_rest = sb.tile([P, HALF], F32, name="q_grouped", align_bytes=64)
-        nc.vector.tensor_copy(a0_rest[:], a_bank[0][:, HALF:I])
-        scatter_vector(0, HALF, I, a0_rest[:])
-        turned0 = look_up(0, "s0", [(0, HALF, a[0][:]), (HALF, I, a0_rest[:])])
-        nc.scalar.copy(a[1][:], a_bank[1][:, 0:SPLIT])
-        scatter_scalar(1, 0, SPLIT)
-        a1_rest = sb.tile([P, I - SPLIT], F32, name="q_grouped", align_bytes=64)
-        nc.vector.tensor_copy(a1_rest[:], a_bank[1][:, SPLIT:I])
-        scatter_vector(1, SPLIT, I, a1_rest[:])
-        turned1 = look_up(1, "s1", [(0, SPLIT, a[1][:]), (SPLIT, I, a1_rest[:])])
-        weigh(0, turned0, "w_grouped0")
-        nc.scalar.copy(a[2][:], a_bank[2][:])
-        scatter_scalar(2, 0, HALF)
-        scatter_scalar(2, HALF, I)
-        turned2 = look_up(2, "w_grouped0", [(0, I, a[2][:])])
-        v_turned = [bank(6, [2, 2, P]), bank(7, [2, 2, P])]
-        picked0 = sb.tile([P, I], BF16, name="picked0", align_bytes=64)
-        pick_values(0, picked0[:], v_turned[0])
-        weigh(1, turned1, "picked0")
-        nc.scalar.copy(a[3][:], a_bank[3][:])
-        scatter_scalar(3, 0, HALF)
-        scatter_scalar(3, HALF, I)
-        turned3 = look_up(3, "picked0", [(0, I, a[3][:])])
-        weigh(2, turned2, "w_grouped2")
-        picked = sb.tile([P, 3 * I], BF16, name="a2", align_bytes=64)
-        pick_values(1, picked[:, 0:I], v_turned[0])
-        pick_values(2, picked[:, I : 2 * I], v_turned[1])
-        pick_values(3, picked[:, 2 * I : 3 * I], v_turned[1])
-        weigh(3, turned3, "w_grouped3")
-        quantize_values(0, v_turned[0], "val_rows3")
-        quantize_values(2, v_turned[1], "v_grouped2")
-
-        o = [sb.tile([P, Q], F32, name=f"o{j}") for j in range(PACK)]
-        for j in range(PACK):
-            sums = bank(j, [Q])
-            weighted_sum(sums[:], j, 0, Q)
-            copy = nc.vector.tensor_copy if j == 1 else nc.scalar.copy
-            copy(o[j][:], sums[:])
-        y = sb.tile([P, PACK, C], F32, name="y")
-        looked_up = sb.tile([P, C], F32, name="looked_up")
-        out_rows = out_0.rearrange("(p j) c -> p j c", j=PACK)
-        for j in range(PACK - 1):
-            nc.vector.tensor_tensor(y[:, j, :], o[j][:].indirect(idx4[:]), gain[:], ALU.mult)
-            if j == 1:
-                nc.sync.dma_start(out_rows[:, 0:2, :], y[:, 0:2, :])
-        nc.scalar.activation(looked_up[:], o[3][:].indirect(idx4[:]), COPY)
-        nc.vector.tensor_tensor(y[:, 3, :], looked_up[:], gain[:], ALU.mult)
-        nc.sync.dma_start(out_rows[:, 2:4, :], y[:, 2:4, :])
+            o = sb.tile([P, Q], F32, name=f"o{j}")
+            nc.scalar.copy(o[:], sums[:])
+            nc.vector.tensor_tensor(y[:, j, :], o[:].indirect(idx4[:]), gain[:], ALU.mult)
+            if j % 2:
+                nc.sync.dma_start(out_rows[:, j - 1 : j + 1, :], y[:, j - 1 : j + 1, :])
 
         y_grouped = sb.tile([P, C, PACK], BF16, name="y_grouped", align_bytes=64)
         y_codes = sb.tile([P, C], U32, name="y_codes", align_bytes=64)
         y_scales = sb.tile([P, C], U8, name="y_scales", align_bytes=64)
-        interleave(nc.vector.tensor_copy, y_grouped[:], y[:])
+        interleave(nc.scalar.copy, y_grouped[:, 0:SCALAR_COLUMNS, :], y[:, :, 0:SCALAR_COLUMNS])
+        interleave(nc.vector.tensor_copy, y_grouped[:, SCALAR_COLUMNS:C, :], y[:, :, SCALAR_COLUMNS:C])
         quantize(y_codes[:], y_scales[:], y_grouped[:])
         nc.sync.dma_start(out_1[0].rearrange("p c t -> p (c t)").bitcast(I32), y_codes[:].bitcast(I32))
         for g in range(4):

@@ -23,6 +23,7 @@ STRIPE = 16
 TILES = Q // P
 HALF = I // 2
 SCALAR_COLUMNS = 96
+SHARE = 160
 
 
 def tile_attend_passedthrough_pickedout_lean_pl_kernel(
@@ -54,7 +55,8 @@ def tile_attend_passedthrough_pickedout_lean_pl_kernel(
         key_words = sb.tile([P, T], U16, name="key_words")
         key_scales = sb.tile([P, T], U8, name="key_scales")
         q_first = sb.tile([P, PACK, P], F32, name="q_first", align_bytes=64)
-        q_rest = sb.tile([P, PACK, Q - P], F32, name="q_rest")
+        q_second = sb.tile([P, PACK, P], F32, name="q_second")
+        q_rest = sb.tile([P, PACK, Q - 2 * P], F32, name="q_rest")
         factor = sb.tile([P, PACK], F32, name="factor")
         gain = sb.tile([P, C], F32, name="gain")
         val_rows = [sb.tile([P, T], F32, name=f"val_rows{j}", align_bytes=64) for j in range(PACK)]
@@ -63,7 +65,7 @@ def tile_attend_passedthrough_pickedout_lean_pl_kernel(
 
         nc.gpsimd.memset(key_scales[:].bitcast(I32), 0)
         for n in range(TILES - 1):
-            nc.vector.memset(f0[n][:], 0.0)
+            nc.vector.memset(f0[n][:].bitcast(I32), 0)
         make_identity(nc, ident[:])
         nc.gpsimd.memset(f0[TILES - 1][:], 0.0)
 
@@ -78,13 +80,14 @@ def tile_attend_passedthrough_pickedout_lean_pl_kernel(
                 key_scales[32 * g : 32 * g + 4, :].bitcast(I32), keys_scales[0, 4 * g : 4 * g + 4, :].bitcast(I32)
             )
         nc.sync.dma_start(key_words[:].bitcast(I32), keys_words[0].bitcast(I32))
-        nc.sync.dma_start(q_rest[:], q_rows[:, :, P:Q])
+        nc.sync.dma_start(q_second[:], q_rows[:, :, P : 2 * P])
+        nc.sync.dma_start(q_rest[:], q_rows[:, :, 2 * P : Q])
+        nc.sync.dma_start(factor[:], slot_factor[0].rearrange("(p t) -> p t", t=PACK))
+        nc.sync.dma_start(idx4[:], offs4)
         for j in range(PACK):
             nc.sync.dma_start(val_rows[j][:], val_dealt[:, j, :])
             if j == 1:
                 nc.sync.dma_start(idx3[:], offs3)
-                nc.sync.dma_start(factor[:], slot_factor[0].rearrange("(p t) -> p t", t=PACK))
-        nc.sync.dma_start(idx4[:], offs4)
         nc.sync.dma_start(gain[:], pgain[0].partition_broadcast(P))
 
         q_codes = sb.tile([P, Q], U32, name="q_codes", align_bytes=64)
@@ -96,7 +99,8 @@ def tile_attend_passedthrough_pickedout_lean_pl_kernel(
         v_scales = sb.tile([P, E], U8, name="v_scales", align_bytes=64)
         k_scales = sb.tile([P, I], U8, name="k_scales", align_bytes=64)
         a_bank = [bank(n, [I]) for n in range(TILES)]
-        a = {n: sb.tile([P, I], F32, name=f"a{n}") for n in (0, 1, 3)}
+        a0_second = bank(4, [HALF])
+        a = {n: sb.tile([P, I], F32, name=f"a{n}") for n in (0, 2, 3)}
 
         def gather_key_words(h, name):
             codes = sb.tile([P, HALF], U16, name=name, align_bytes=64)
@@ -111,7 +115,7 @@ def tile_attend_passedthrough_pickedout_lean_pl_kernel(
         def score(n, h):
             rows = slice(n * P, (n + 1) * P)
             nc.tensor.matmul_mx(
-                out=a_bank[n][:, h * HALF : (h + 1) * HALF],
+                out=a0_second[:] if (n, h) == (0, 1) else a_bank[n][:, h * HALF : (h + 1) * HALF],
                 lhsT=q_codes[:, rows].bitcast(FP8X4),
                 lhsT_scale=q_scales[:, rows],
                 rhs=k_codes[h][:].bitcast(FP4X4),
@@ -169,28 +173,30 @@ def tile_attend_passedthrough_pickedout_lean_pl_kernel(
         scatter_scalar(0, 0, HALF)
         k_codes.append(gather_key_words(1, "q_first"))
         score(0, 1)
-        nc.scalar.copy(a[0][:, HALF:I], a_bank[0][:, HALF:I])
+        nc.scalar.copy(a[0][:, HALF:I], a0_second[:])
         scatter_scalar(0, HALF, I)
-        grouped = round_queries(nc.vector.tensor_copy, q_rest[:], "q_grouped1")
-        quantize(q_codes[:, P:Q], q_scales[:, P:Q], grouped[:])
-        for n in (2, 1, 3):
+        for copy, src, lo, hi in ((nc.scalar.copy, q_second, P, 2 * P), (nc.vector.tensor_copy, q_rest, 2 * P, Q)):
+            grouped = round_queries(copy, src[:], f"q_grouped{lo}")
+            quantize(q_codes[:, lo:hi], q_scales[:, lo:hi], grouped[:])
+        for n in range(1, TILES):
             score(n, 0)
             score(n, 1)
         v_turned = [bank(4, [2, 2, P]), bank(5, [2, 2, P])]
+        a[1] = sb.tile([P, I], F32, name="q_grouped256", align_bytes=64)
+        nc.vector.tensor_copy(a[1][:], a_bank[1][:])
+        nc.vector.tensor_copy(f0[1][:].indirect(idx2[:]), a[1][:])
+        nc.scalar.copy(a[2][:], a_bank[2][:])
+        nc.scalar.copy(a[3][:], a_bank[3][:])
+        scatter_scalar(2, 0, HALF)
+        scatter_scalar(2, HALF, I)
+        nc.vector.tensor_copy(f0[3][:].indirect(entries(idx2, 0, SHARE)), a[3][:, 0:SHARE])
+        scatter_scalar(3, SHARE, I)
         pick_values(0, "picked0")
-        a[2] = sb.tile([P, I], F32, name="val_rows0", align_bytes=64)
-        nc.vector.tensor_copy(a[2][:], a_bank[2][:])
-        nc.vector.tensor_copy(a[3][:], a_bank[3][:])
-        nc.vector.tensor_copy(f0[2][:].indirect(idx2[:]), a[2][:])
-        nc.scalar.copy(a[1][:], a_bank[1][:])
-        for n in (1, 3):
-            scatter_scalar(n, 0, HALF)
-            scatter_scalar(n, HALF, I)
-        turned = {n: look_up(n) for n in (0, 2, 1, 3)}
-        for n in turned:
+        turned = [look_up(n) for n in range(TILES)]
+        for n in range(TILES):
             weigh(n, turned[n])
         quantize(w_codes[:], w_scales[:], w_grouped[:])
-        pick_values(1, "val_rows0")
+        pick_values(1, "q_grouped256")
         pick_values(2, "picked2")
         pick_values(3, "picked3")
         quantize_values(0, "val_rows3")

@@ -55,7 +55,7 @@ def tile_attend_passedthrough_pickedout_lean_pl_kernel(
         key_words = sb.tile([P, T], U16, name="key_words")
         key_scales = sb.tile([P, T], U8, name="key_scales")
         q_first = sb.tile([P, PACK, P], F32, name="q_first", align_bytes=64)
-        q_second = sb.tile([P, PACK, P], F32, name="q_second")
+        q_second = sb.tile([P, PACK, P], F32, name="q_second", align_bytes=64)
         q_rest = sb.tile([P, PACK, Q - 2 * P], F32, name="q_rest")
         factor = sb.tile([P, PACK], F32, name="factor")
         gain = sb.tile([P, C], F32, name="gain")
@@ -100,7 +100,7 @@ def tile_attend_passedthrough_pickedout_lean_pl_kernel(
         k_scales = sb.tile([P, I], U8, name="k_scales", align_bytes=64)
         a_bank = [bank(n, [I]) for n in range(TILES)]
         a0_second = bank(4, [HALF])
-        a = {n: sb.tile([P, I], F32, name=f"a{n}") for n in (0, 2, 3)}
+        a = {n: sb.tile([P, I], F32, name=f"a{n}") for n in (2, 3)}
 
         def gather_key_words(h, name):
             codes = sb.tile([P, HALF], U16, name=name, align_bytes=64)
@@ -169,15 +169,17 @@ def tile_attend_passedthrough_pickedout_lean_pl_kernel(
         grouped = round_queries(nc.scalar.copy, q_first[:], "q_grouped0")
         quantize(q_codes[:, 0:P], q_scales[:, 0:P], grouped[:])
         score(0, 0)
+        grouped_second = round_queries(nc.scalar.copy, q_second[:], "q_grouped1")
+        a[0] = sb.tile([P, I], F32, name="q_second", align_bytes=64)
         nc.scalar.copy(a[0][:, 0:HALF], a_bank[0][:, 0:HALF])
         scatter_scalar(0, 0, HALF)
         k_codes.append(gather_key_words(1, "q_first"))
         score(0, 1)
         nc.scalar.copy(a[0][:, HALF:I], a0_second[:])
         scatter_scalar(0, HALF, I)
-        for copy, src, lo, hi in ((nc.scalar.copy, q_second, P, 2 * P), (nc.vector.tensor_copy, q_rest, 2 * P, Q)):
-            grouped = round_queries(copy, src[:], f"q_grouped{lo}")
-            quantize(q_codes[:, lo:hi], q_scales[:, lo:hi], grouped[:])
+        quantize(q_codes[:, P : 2 * P], q_scales[:, P : 2 * P], grouped_second[:])
+        grouped = round_queries(nc.vector.tensor_copy, q_rest[:], "q_grouped256")
+        quantize(q_codes[:, 2 * P : Q], q_scales[:, 2 * P : Q], grouped[:])
         for n in range(1, TILES):
             score(n, 0)
             score(n, 1)

from contextlib import ExitStack

import concourse.mybir as mybir
from concourse.masks import make_identity

D, T, I, Q, E, Z, C = 512, 2048, 512, 512, 512, 1024, 256
FLOPS = 2 * D * Q * I + 2 * I * E * Q

F32 = mybir.dt.float32
BF16 = mybir.dt.bfloat16
I32 = mybir.dt.int32
U32 = mybir.dt.uint32
U16 = mybir.dt.uint16
U8 = mybir.dt.uint8
FP8X4 = mybir.dt.float8_e4m3fn_x4
FP4X4 = mybir.dt.float4_e2m1fn_x4
ALU = mybir.AluOpType
COPY = mybir.ActivationFunctionType.Copy

P = 128
PACK = 4
STRIPE = 16
TILES = Q // P
HALF = I // 2
SCALAR_COLUMNS = 96
SHARE = 160


def tile_attend_passedthrough_pickedout_lean_pl_kernel(
    tc, query, keys_words, keys_scales, slot_factor, vals, pgain, offs, offs2, offs3, offs4, out_0, out_1, out_2
):
    nc = tc.nc
    with ExitStack() as ctx:
        lists = ctx.enter_context(tc.tile_pool(name="lists", bufs=1))
        sb = ctx.enter_context(tc.tile_pool(name="sb", bufs=1))
        psum = ctx.enter_context(tc.psum_pool(name="psum", bufs=1))

        def bank(b, shape):
            return psum.tile([P] + shape, F32, name=f"bank{b}")

        def entries(tile, a, b):
            return tile[:, a // STRIPE : b // STRIPE]

        def interleave(copy, dst, src):
            copy(dst.rearrange("p (c i) t -> p c t i", i=4), src.rearrange("p t (c i) -> p c t i", i=4))

        def quantize(codes, scales, grouped):
            nc.vector.quantize_mx(out=codes.bitcast(FP8X4), scales=scales, in_=grouped.rearrange("p c t -> p (c t)"))

        idx = lists.tile([P, I // STRIPE], U16, name="idx")
        idx2 = lists.tile([P, I // STRIPE], U16, name="idx2")
        idx3 = lists.tile([P, I // STRIPE], U16, name="idx3")
        idx4 = lists.tile([P, C // STRIPE], U16, name="idx4")

        key_words = sb.tile([P, T], U16, name="key_words")
        key_scales = sb.tile([P, T], U8, name="key_scales")
        q_first = sb.tile([P, PACK, P], F32, name="q_first", align_bytes=64)
        q_second = sb.tile([P, PACK, P], F32, name="q_second", align_bytes=64)
        q_rest = sb.tile([P, PACK, Q - 2 * P], F32, name="q_rest")
        factor = sb.tile([P, PACK], F32, name="factor")
        gain = sb.tile([P, C], F32, name="gain")
        val_rows = [sb.tile([P, T], F32, name=f"val_rows{j}", align_bytes=64) for j in range(PACK)]
        f0 = [sb.tile([P, Z], F32, name=f"f0_{n}", align_bytes=64) for n in range(TILES)]
        ident = sb.tile([P, P], F32, name="ident")

        nc.gpsimd.memset(key_scales[:].bitcast(I32), 0)
        for n in range(TILES - 1):
            nc.vector.memset(f0[n][:].bitcast(I32), 0)
        make_identity(nc, ident[:])
        nc.gpsimd.memset(f0[TILES - 1][:], 0.0)

        q_rows = query.rearrange("(p j) q -> p j q", j=PACK)
        val_dealt = vals.rearrange("(p j) t -> p j t", j=PACK)
        nc.sync.dma_start(idx[:], offs)
        nc.sync.dma_start(idx2[:], offs2)
        nc.scalar.dma_start(q_first[:], q_rows[:, :, 0:P])
        for g in range(4):
            queue = nc.sync if g % 2 == 0 else nc.scalar
            queue.dma_start(
                key_scales[32 * g : 32 * g + 4, :].bitcast(I32), keys_scales[0, 4 * g : 4 * g + 4, :].bitcast(I32)
            )
        nc.sync.dma_start(key_words[:].bitcast(I32), keys_words[0].bitcast(I32))
        nc.sync.dma_start(q_second[:], q_rows[:, :, P : 2 * P])
        nc.sync.dma_start(q_rest[:], q_rows[:, :, 2 * P : Q])
        nc.sync.dma_start(factor[:], slot_factor[0].rearrange("(p t) -> p t", t=PACK))
        nc.sync.dma_start(idx4[:], offs4)
        for j in range(PACK):
            nc.sync.dma_start(val_rows[j][:], val_dealt[:, j, :])
            if j == 1:
                nc.sync.dma_start(idx3[:], offs3)
        nc.sync.dma_start(gain[:], pgain[0].partition_broadcast(P))

        q_codes = sb.tile([P, Q], U32, name="q_codes", align_bytes=64)
        q_scales = sb.tile([P, Q], U8, name="q_scales", align_bytes=64)
        w_codes = sb.tile([P, Q], U32, name="w_codes", align_bytes=64)
        w_scales = sb.tile([P, Q], U8, name="w_scales", align_bytes=64)
        w_grouped = sb.tile([P, Q, PACK], BF16, name="w_grouped", align_bytes=64)
        v_codes = sb.tile([P, E], U32, name="v_codes", align_bytes=64)
        v_scales = sb.tile([P, E], U8, name="v_scales", align_bytes=64)
        k_scales = sb.tile([P, I], U8, name="k_scales", align_bytes=64)
        a_bank = [bank(n, [I]) for n in range(TILES)]
        a0_second = bank(4, [HALF])
        a = {n: sb.tile([P, I], F32, name=f"a{n}") for n in (2, 3)}

        def gather_key_words(h, name):
            codes = sb.tile([P, HALF], U16, name=name, align_bytes=64)
            nc.vector.tensor_copy(codes[:], key_words[:].indirect(entries(idx, h * HALF, (h + 1) * HALF)))
            return codes

        def round_queries(copy, src, name):
            grouped = sb.tile([P, src.shape[2], PACK], BF16, name=name, align_bytes=64)
            interleave(copy, grouped[:], src)
            return grouped

        def score(n, h):
            rows = slice(n * P, (n + 1) * P)
            nc.tensor.matmul_mx(
                out=a0_second[:] if (n, h) == (0, 1) else a_bank[n][:, h * HALF : (h + 1) * HALF],
                lhsT=q_codes[:, rows].bitcast(FP8X4),
                lhsT_scale=q_scales[:, rows],
                rhs=k_codes[h][:].bitcast(FP4X4),
                rhs_scale=k_scales[:, h * HALF : (h + 1) * HALF],
                start=True,
                stop=True,
            )

        def scatter_scalar(n, lo, hi):
            nc.scalar.activation(f0[n][:].indirect(entries(idx2, lo, hi)), a[n][:, lo:hi], COPY)

        def look_up(n):
            s = sb.tile([P, I], F32, name=f"s{n}")
            nc.vector.tensor_tensor(s[:], f0[n][:].indirect(idx3[:]), a[n][:], ALU.add)
            turned = bank(n, [PACK, P])
            for t in range(PACK):
                nc.tensor.transpose(turned[:, t, :], s[:, t:I:PACK], ident[:])
            return turned

        def weigh(n, turned):
            nc.vector.scalar_tensor_tensor(
                out=w_grouped[:, n * P : (n + 1) * P, :],
                in0=turned[:].rearrange("p t q -> p q t"),
                scalar=0.0,
                in1=factor[:].unsqueeze(1).to_broadcast([P, P, PACK]),
                op0=ALU.max,
                op1=ALU.mult,
            )

        def pick_values(j, name):
            picked = sb.tile([P, I], BF16, name=name, align_bytes=64)
            if j >= 1:
                nc.scalar.activation(picked[:], val_rows[j][:].indirect(idx[:]), COPY)
            else:
                nc.vector.tensor_copy(picked[:], val_rows[j][:].indirect(idx[:]))
            pairs = picked[:].bitcast(F32)
            for u in range(2):
                nc.tensor.transpose(v_turned[j // 2][:, j % 2, u, :], pairs[:, u : I // 2 : 2], ident[:])

        def quantize_values(j, name):
            grouped = sb.tile([P, 2 * P, PACK], BF16, name=name, align_bytes=64)
            nc.scalar.copy(
                grouped[:].bitcast(F32).rearrange("p (j m) u -> p j m u", j=2),
                v_turned[j // 2][:].rearrange("p j u m -> p j m u"),
            )
            cols = slice(j * P, (j + 2) * P)
            quantize(v_codes[:, cols], v_scales[:, cols], grouped[:])

        nc.vector.tensor_copy(k_scales[:], key_scales[:].indirect(idx[:]))
        k_codes = [gather_key_words(0, "k_codes")]
        grouped = round_queries(nc.scalar.copy, q_first[:], "q_grouped0")
        quantize(q_codes[:, 0:P], q_scales[:, 0:P], grouped[:])
        score(0, 0)
        grouped_second = round_queries(nc.scalar.copy, q_second[:], "q_grouped1")
        a[0] = sb.tile([P, I], F32, name="q_second", align_bytes=64)
        nc.scalar.copy(a[0][:, 0:HALF], a_bank[0][:, 0:HALF])
        scatter_scalar(0, 0, HALF)
        k_codes.append(gather_key_words(1, "q_first"))
        score(0, 1)
        nc.scalar.copy(a[0][:, HALF:I], a0_second[:])
        scatter_scalar(0, HALF, I)
        quantize(q_codes[:, P : 2 * P], q_scales[:, P : 2 * P], grouped_second[:])
        grouped = round_queries(nc.vector.tensor_copy, q_rest[:], "q_grouped256")
        quantize(q_codes[:, 2 * P : Q], q_scales[:, 2 * P : Q], grouped[:])
        for n in range(1, TILES):
            score(n, 0)
            score(n, 1)
        v_turned = [bank(4, [2, 2, P]), bank(5, [2, 2, P])]
        a[1] = sb.tile([P, I], F32, name="q_grouped256", align_bytes=64)
        nc.vector.tensor_copy(a[1][:], a_bank[1][:])
        nc.vector.tensor_copy(f0[1][:].indirect(idx2[:]), a[1][:])
        nc.scalar.copy(a[2][:], a_bank[2][:])
        nc.scalar.copy(a[3][:], a_bank[3][:])
        scatter_scalar(2, 0, HALF)
        scatter_scalar(2, HALF, I)
        nc.vector.tensor_copy(f0[3][:].indirect(entries(idx2, 0, SHARE)), a[3][:, 0:SHARE])
        scatter_scalar(3, SHARE, I)
        pick_values(0, "picked0")
        turned = [look_up(n) for n in range(TILES)]
        for n in range(TILES):
            weigh(n, turned[n])
        quantize(w_codes[:], w_scales[:], w_grouped[:])
        pick_values(1, "q_grouped256")
        pick_values(2, "picked2")
        pick_values(3, "picked3")
        quantize_values(0, "val_rows3")
        quantize_values(2, "v_grouped")

        y = sb.tile([P, PACK, C], F32, name="y")
        out_rows = out_0.rearrange("(p j) c -> p j c", j=PACK)
        for j in range(PACK):
            sums = bank((6, 7, 0, 1)[j], [Q])
            cols = slice(j * P, (j + 1) * P)
            nc.tensor.matmul_mx(
                out=sums[:],
                lhsT=v_codes[:, cols].bitcast(FP8X4),
                lhsT_scale=v_scales[:, cols],
                rhs=w_codes[:].bitcast(FP8X4),
                rhs_scale=w_scales[:],
                start=True,
                stop=True,
            )
            o = sb.tile([P, Q], F32, name=f"o{j}")
            nc.scalar.copy(o[:], sums[:])
            nc.vector.tensor_tensor(y[:, j, :], o[:].indirect(idx4[:]), gain[:], ALU.mult)
            if j % 2:
                nc.sync.dma_start(out_rows[:, j - 1 : j + 1, :], y[:, j - 1 : j + 1, :])

        y_grouped = sb.tile([P, C, PACK], BF16, name="y_grouped", align_bytes=64)
        y_codes = sb.tile([P, C], U32, name="y_codes", align_bytes=64)
        y_scales = sb.tile([P, C], U8, name="y_scales", align_bytes=64)
        interleave(nc.scalar.copy, y_grouped[:, 0:SCALAR_COLUMNS, :], y[:, :, 0:SCALAR_COLUMNS])
        interleave(nc.vector.tensor_copy, y_grouped[:, SCALAR_COLUMNS:C, :], y[:, :, SCALAR_COLUMNS:C])
        quantize(y_codes[:], y_scales[:], y_grouped[:])
        nc.sync.dma_start(out_1[0].rearrange("p c t -> p (c t)").bitcast(I32), y_codes[:].bitcast(I32))
        for g in range(4):
            queue = nc.sync if g % 2 == 0 else nc.scalar
            queue.dma_start(
                out_2[0, 4 * g : 4 * g + 4, :].bitcast(I32), y_scales[32 * g : 32 * g + 4, :].bitcast(I32)
            )
